import numpy as np
import ml_dtypes


def mxq(x, axis, fmt="e4m3"):
    dtype, down = {"e4m3": (ml_dtypes.float8_e4m3fn, 7), "e5m2": (ml_dtypes.float8_e5m2, 14)}[fmt]
    v = np.moveaxis(np.asarray(x, np.float32).astype(ml_dtypes.bfloat16).astype(np.float64), axis, -1)
    blocks = v.reshape(v.shape[:-1] + (-1, 32))
    amax = np.abs(blocks).max(-1, keepdims=True)
    byte = np.maximum(np.where(amax > 0, np.frexp(amax)[1] - 1 + 127, 0) - down, 1)
    scale = np.exp2(byte - 127.0)
    codes = (blocks / scale).astype(np.float32).astype(dtype).astype(np.float64)
    return np.moveaxis((codes * scale).reshape(v.shape), -1, axis)


WIDE = False


def mx_kscale(k):
    if not WIDE:
        return np.ones(k)
    levels = np.array([10, -10, 5, -5, 0])
    if k % 512:
        return np.exp2(np.random.permutation(np.resize(levels, k // 32))).repeat(32)
    a = np.empty((k // 512, 16))
    for p in range(k // 512):
        a[p, :8] = np.random.permutation(np.resize(levels, 8))
        for g in range(8):
            far = levels[np.abs(levels - a[p, g]) >= 10]
            a[p, g + 8] = far[np.random.randint(len(far))]
    return np.exp2(a.ravel()).repeat(32)


BF16 = ml_dtypes.bfloat16


def bf(x):
    return np.asarray(x, np.float32).astype(BF16)


def f64(x):
    return np.asarray(x).astype(np.float64)

E4M3FN = np.array([(-1.0 if i & 128 else 1.0) * ((1.0 + (i & 7) / 8.0) * 2.0 ** (((i >> 3) & 15) - 7) if i & 120 else (i & 7) * 2.0 ** -9) for i in range(256)])


def e4m3fn_bytes(y):
    return np.clip(np.asarray(y, np.float64), -448.0, 448.0).astype(np.float32).astype(ml_dtypes.float8_e4m3fn).view(np.uint8)


def e4m3fn_values(b):
    return E4M3FN[b]


T, K, R = 1536, 2048, 512


def setup_inputs():
    s, t = mx_kscale(K), mx_kscale(R)
    wd = np.random.standard_normal((K, R)) / np.sqrt(K) / s[:, None]
    wu = np.random.standard_normal((R, K)) * np.sqrt(2.0 / R) / t[:, None]
    wd_scale = (np.abs(wd).max(axis=1, keepdims=True) / 448.0).astype(np.float32)
    wu_scale = (np.abs(wu).max(axis=1, keepdims=True) / 448.0).astype(np.float32)
    return {"x": bf(np.random.standard_normal((T, K))),
            "a": bf((1.0 + 0.1 * np.random.standard_normal(K)) * s),
            "wd_bytes": e4m3fn_bytes(wd / wd_scale.astype(np.float64)),
            "wd_scale": wd_scale,
            "g": bf((1.0 + 0.1 * np.random.standard_normal(R)) * t),
            "wu_bytes": e4m3fn_bytes(wu / wu_scale.astype(np.float64)),
            "wu_scale": wu_scale}


def reference(x, a, wd_bytes, wd_scale, g, wu_bytes, wu_scale):
    wd = e4m3fn_values(wd_bytes) * np.repeat(f64(wd_scale), R, axis=1)
    wu = e4m3fn_values(wu_bytes) * np.repeat(f64(wu_scale), K, axis=1)
    xa = f64(x) * f64(a)
    d = mxq(xa, 1, "e4m3") @ mxq(wd, 0, "e4m3")
    h = np.maximum(d, 0.0) * f64(g)
    u = mxq(h, 1, "e4m3") @ mxq(wu, 0, "e4m3")
    return f64(x) + u

@@ -1,0 +1,298 @@
+from contextlib import ExitStack
+
+import concourse.mybir as mybir
+from concourse.masks import make_identity
+
+T, K, R = 1536, 2048, 512
+FLOPS = 2 * T * K * R * 2
+
+F32 = mybir.dt.float32
+BF16 = mybir.dt.bfloat16
+U32 = mybir.dt.uint32
+U8 = mybir.dt.uint8
+FP8 = mybir.dt.float8_e4m3fn
+FP8X4 = mybir.dt.float8_e4m3fn_x4
+ADD = mybir.AluOpType.add
+MULT = mybir.AluOpType.mult
+MAX = mybir.AluOpType.max
+COPY = mybir.ActivationFunctionType.Copy
+
+P = 128
+NT = T // P
+G1 = K // 512
+NC = 512
+CH = K // NC
+LAG = 2
+AHEAD = 3
+
+
+def tile_fp8_bottleneck_adapter_d3_kernel(tc, x, a, wd_bytes, wd_scale, g, wu_bytes, wu_scale, out):
+    nc = tc.nc
+    with ExitStack() as ctx:
+        keep = ctx.enter_context(tc.tile_pool(name="keep", bufs=1))
+        xpool = ctx.enter_context(tc.tile_pool(name="xpool", bufs=NT))
+        wpool = ctx.enter_context(tc.tile_pool(name="wpool", bufs=4))
+        xapool = ctx.enter_context(tc.tile_pool(name="xapool", bufs=3))
+        xqpool = ctx.enter_context(tc.tile_pool(name="xqpool", bufs=4))
+        hpool = ctx.enter_context(tc.tile_pool(name="hpool", bufs=5))
+        opool = ctx.enter_context(tc.tile_pool(name="opool", bufs=3))
+        ps_x = ctx.enter_context(tc.psum_pool(name="ps_x", bufs=3))
+        ps_d = ctx.enter_context(tc.psum_pool(name="ps_d", bufs=1))
+        ps_u = ctx.enter_context(tc.psum_pool(name="ps_u", bufs=1))
+
+        ident = keep.tile([P, P], F32, name="ident", align_bytes=64)
+        wd_sc = keep.tile([P, G1, 4], F32, name="wd_sc")
+        wu_sc = keep.tile([P, 4], F32, name="wu_sc")
+        a_sb = keep.tile([P, G1, 4], BF16, name="a_sb")
+        g_sb = keep.tile([P, 4], BF16, name="g_sb")
+        wd_raw = [keep.tile([P, 4, R], U8, name=f"wd_raw{q}", align_bytes=64) for q in range(G1)]
+        wu_raw = [keep.tile([P, 4, K // 2], U8, name=f"wu_raw{q}", align_bytes=64) for q in range(2)]
+        wd_q = [keep.tile([P, R], U32, name=f"wd_q{q}", align_bytes=64) for q in range(G1)]
+        wd_s = [keep.tile([P, R], U8, name=f"wd_s{q}", align_bytes=64) for q in range(G1)]
+        wu_q = [keep.tile([P, NC], U32, name=f"wu_q{q}", align_bytes=64) for q in range(CH)]
+        wu_s = [keep.tile([P, NC], U8, name=f"wu_s{q}", align_bytes=64) for q in range(CH)]
+
+        ctx.enter_context(tc.manual_schedule())
+
+        nc.scalar.dma_start(out=wd_sc[:], in_=wd_scale.rearrange("(g p j) o -> p g (j o)", p=P, j=4))
+        nc.scalar.dma_start(out=a_sb[:], in_=a.rearrange("(g p j) -> p g j", p=P, j=4))
+        nc.scalar.dma_start(out=wu_sc[:], in_=wu_scale.rearrange("(p j) o -> p (j o)", j=4))
+        nc.scalar.dma_start(out=g_sb[:], in_=g.rearrange("(p j) -> p j", j=4))
+        make_identity(nc, ident[:])
+
+        xs = {}
+
+        def load_x(i):
+            t = xpool.tile([P, K], BF16, name="xt_in", align_bytes=64)
+            nc.sync.dma_start(out=t[:], in_=x[i * P : (i + 1) * P, :])
+            xs[i] = t
+
+        wd_view = wd_bytes.rearrange("(g p j) r -> g p j r", p=P, j=4)
+        wu_view = wu_bytes.rearrange("(p j) n -> p j n", j=4)
+        for q in range(G1):
+            nc.sync.dma_start(out=wd_raw[q][:], in_=wd_view[q])
+        load_x(0)
+        nc.sync.dma_start(out=wu_raw[0][:], in_=wu_view[:, :, 0 : K // 2])
+        load_x(1)
+        nc.sync.dma_start(out=wu_raw[1][:], in_=wu_view[:, :, K // 2 : K])
+        for i in range(2, NT):
+            load_x(i)
+
+        wide = {}
+        grp = {}
+
+        def widen(kind, q, eng):
+            t = wpool.tile([P, 4, NC], BF16, name="wide", align_bytes=64)
+            for j in range(4):
+                if kind == "d":
+                    src, sc = wd_raw[q][:, j, :], wd_sc[:, q, j : j + 1]
+                else:
+                    src, sc = wu_raw[q // 2][:, j, (q % 2) * NC : (q % 2 + 1) * NC], wu_sc[:, j : j + 1]
+                src = src.bitcast(FP8)
+                if eng == "S":
+                    nc.scalar.activation(out=t[:, j, :], in_=src, func=COPY, scale=sc)
+                else:
+                    nc.vector.tensor_scalar(out=t[:, j, :], in0=src, scalar1=sc, scalar2=None, op0=MULT)
+            wide[kind, q] = t
+
+        def interleave(kind, q, eng):
+            t = wpool.tile([P, NC, 4], BF16, name="grp", align_bytes=64)
+            if kind == "d":
+                dst = t[:].rearrange("p (t m) j -> p t m j", t=4)
+                src = wide[kind, q][:].rearrange("p j (m t) -> p t m j", t=4)
+            else:
+                dst = t[:]
+                src = wide[kind, q][:].rearrange("p j n -> p n j")
+            if eng == "V":
+                nc.vector.tensor_copy(out=dst, in_=src)
+            elif eng == "S":
+                nc.scalar.copy(out=dst, in_=src)
+            else:
+                nc.gpsimd.tensor_scalar(out=dst, in0=src, scalar1=1.0, scalar2=0.0, op0=MULT, op1=ADD)
+            grp[kind, q] = t
+
+        def quantize_w(kind, q):
+            codes, scales = (wd_q[q], wd_s[q]) if kind == "d" else (wu_q[q], wu_s[q])
+            nc.vector.quantize_mx(
+                out=codes[:].bitcast(FP8X4),
+                scales=scales[:],
+                in_=grp[kind, q][:].rearrange("p n j -> p (n j)"),
+            )
+
+        xt_ps = {}
+        xa = {}
+        xq = {}
+        d_ps = {}
+        hg = {}
+        hq = {}
+        u_ps = {}
+        osb = {}
+
+        def on_vector(i):
+            if i == NT - 1:
+                return 3
+            return 1 if i % 2 == 1 and i < NT - 2 else 2
+
+        def transposes(i):
+            words = xs[i][:].bitcast(F32)
+            for b in range(2):
+                pt = ps_x.tile([P, 2, 2, P], F32, name="xt")
+                for u in range(2):
+                    for gl in range(2):
+                        q = 2 * b + gl
+                        nc.tensor.transpose(pt[:, u, gl, :], words[:, 256 * q + u : 256 * (q + 1) : 2], ident[:])
+                xt_ps[i, b] = pt
+
+        def exit_x(i, b):
+            if b == 0:
+                xa[i] = xapool.tile([P, G1, P, 2, 2], BF16, name="xa", align_bytes=64)
+            src = xt_ps[i, b][:].rearrange("p u g r -> p (u g r)").bitcast(BF16).rearrange("p (u g r e) -> p g r u e", u=2, g=2, e=2)
+            fac = a_sb[:, 2 * b : 2 * b + 2, :].rearrange("p g (u e) -> p g u e", e=2).unsqueeze(2).to_broadcast([P, 2, P, 2, 2])
+            nc.vector.tensor_tensor(out=xa[i][:, 2 * b : 2 * b + 2], in0=src, in1=fac, op=MULT)
+
+        def quantize_x(i):
+            codes = xqpool.tile([P, G1, P], U32, name="xq", align_bytes=64)
+            scales = xqpool.tile([P, G1, P], U8, name="xqs", align_bytes=64)
+            nc.vector.quantize_mx(
+                out=codes[:].rearrange("p g r -> p (g r)").bitcast(FP8X4),
+                scales=scales[:].rearrange("p g r -> p (g r)"),
+                in_=xa[i][:].rearrange("p g r u e -> p (g r u e)"),
+            )
+            xq[i] = (codes, scales)
+
+        def stage1(i):
+            pt = ps_d.tile([P, 4, P], F32, name="d")
+            codes, scales = xq[i]
+            for t in range(4):
+                for q in range(G1):
+                    nc.tensor.matmul_mx(
+                        out=pt[:, t, :],
+                        lhsT=wd_q[q][:, t * P : (t + 1) * P].bitcast(FP8X4),
+                        lhsT_scale=wd_s[q][:, t * P : (t + 1) * P],
+                        rhs=codes[:, q, :].bitcast(FP8X4),
+                        rhs_scale=scales[:, q, :],
+                        start=(q == 0),
+                        stop=(q == G1 - 1),
+                    )
+            d_ps[i] = pt
+
+        def exit_d(i):
+            t = hpool.tile([P, P, 4], BF16, name="hg", align_bytes=64)
+            nc.vector.scalar_tensor_tensor(
+                out=t[:],
+                in0=d_ps[i][:].rearrange("p t n -> p n t"),
+                scalar=0.0,
+                in1=g_sb[:].unsqueeze(1).to_broadcast([P, P, 4]),
+                op0=MAX,
+                op1=MULT,
+            )
+            hg[i] = t
+
+        def quantize_h(i):
+            codes = hpool.tile([P, P], U32, name="hq", align_bytes=64)
+            scales = hpool.tile([P, P], U8, name="hqs", align_bytes=64)
+            nc.vector.quantize_mx(
+                out=codes[:].bitcast(FP8X4), scales=scales[:], in_=hg[i][:].rearrange("p n t -> p (n t)")
+            )
+            hq[i] = (codes, scales)
+
+        def stage2(i, c):
+            pt = ps_u.tile([P, NC], F32, name=f"u{c}")
+            codes, scales = hq[i]
+            nc.tensor.matmul_mx(
+                out=pt[:],
+                lhsT=codes[:].bitcast(FP8X4),
+                lhsT_scale=scales[:],
+                rhs=wu_q[c][:].bitcast(FP8X4),
+                rhs_scale=wu_s[c][:],
+                start=True,
+                stop=True,
+            )
+            u_ps[i, c] = pt
+
+        def exit_u(i, c):
+            h = c // 2
+            cols = slice(c * NC, (c + 1) * NC)
+            if c % 2 == 0:
+                osb[i, h] = opool.tile([P, 2 * NC], F32, name=f"o{h}", align_bytes=64)
+            dst = osb[i, h][:, (c % 2) * NC : (c % 2 + 1) * NC]
+            if c < on_vector(i):
+                nc.vector.tensor_tensor(out=dst, in0=u_ps[i, c][:], in1=xs[i][:, cols], op=ADD)
+            else:
+                nc.scalar.copy(out=dst, in_=u_ps[i, c][:])
+
+        def finish(i, h):
+            lo = max(on_vector(i) - 2 * h, 0) * NC
+            base = h * 2 * NC
+            if lo < 2 * NC:
+                part = osb[i, h][:, lo : 2 * NC]
+                nc.gpsimd.tensor_tensor(out=part, in0=part, in1=xs[i][:, base + lo : base + 2 * NC], op=ADD)
+            rows = slice(i * P, (i + 1) * P)
+            if i == NT - 1:
+                for s in range(0, 2 * NC, NC):
+                    nc.sync.dma_start(out=out[rows, base + s : base + s + NC], in_=osb[i, h][:, s : s + NC])
+            else:
+                nc.sync.dma_start(out=out[rows, base : base + 2 * NC], in_=osb[i, h][:])
+
+        def step(i):
+            j = i - LAG
+            if 0 <= j < NT:
+                for c in range(CH):
+                    stage2(j, c)
+            if 0 <= i < NT:
+                stage1(i)
+            if 0 <= i + AHEAD < NT:
+                transposes(i + AHEAD)
+            k = i + AHEAD - 1
+            if 0 <= k < NT:
+                exit_x(k, 0)
+            if 0 <= j < NT:
+                exit_u(j, 0)
+            if 0 <= k < NT:
+                exit_x(k, 1)
+            if 0 <= j < NT:
+                exit_u(j, 1)
+                finish(j, 0)
+                exit_u(j, 2)
+                exit_u(j, 3)
+                finish(j, 1)
+            if 0 <= i < NT:
+                exit_d(i)
+            if 0 <= k < NT:
+                quantize_x(k)
+            if 0 <= i < NT:
+                quantize_h(i)
+
+        widen("d", 0, "S")
+        widen("d", 1, "V")
+        interleave("d", 1, "V")
+        interleave("d", 0, "G")
+        transposes(0)
+        widen("d", 2, "S")
+        quantize_w("d", 1)
+        exit_x(0, 0)
+        exit_x(0, 1)
+        interleave("d", 2, "G")
+        transposes(1)
+        quantize_x(0)
+        quantize_w("d", 0)
+        widen("d", 3, "S")
+        exit_x(1, 0)
+        exit_x(1, 1)
+        interleave("d", 3, "V")
+        quantize_x(1)
+        quantize_w("d", 2)
+        quantize_w("d", 3)
+        transposes(2)
+        for i in range(NT + LAG):
+            if i == 0:
+                for c in range(CH):
+                    widen("u", c, "S")
+                    interleave("u", c, "S" if c == CH - 1 else "G")
+                quantize_w("u", 0)
+            if i == 1:
+                quantize_w("u", 1)
+            if i == LAG:
+                quantize_w("u", 2)
+                quantize_w("u", 3)
+            step(i)

@@ -22,8 +22,13 @@ NT = T // P
 G1 = K // 512
 NC = 512
 CH = K // NC
-LAG = 2
-AHEAD = 3
+LAG = 4
+AHEAD = 8
+IL = {"d0": "V", "d1": "V", "d2": "V", "d3": "S", "u0": "S", "u1": "S", "u2": "S", "u3": "S"}
+WID = {"d1": "V"}
+S_ORDER = "wd0 wd2 wd3 id3 wu0 iu0 wu1 iu1 wu2 iu2 wu3 iu3"
+V_AT = {0: "wd1 id1 id0", 2: "qd1", 4: "id2", 5: "qd2", 6: "qd0 qd3", 8: "qu0", 9: "qu1", 10: "qu2", 11: "qu3"}
+NV = [3]*12
 
 
 def tile_fp8_bottleneck_adapter_d3_kernel(tc, x, a, wd_bytes, wd_scale, g, wu_bytes, wu_scale, out):
@@ -33,12 +38,11 @@ def tile_fp8_bottleneck_adapter_d3_kernel(tc, x, a, wd_bytes, wd_scale, g, wu_by
         xpool = ctx.enter_context(tc.tile_pool(name="xpool", bufs=NT))
         wpool = ctx.enter_context(tc.tile_pool(name="wpool", bufs=4))
         xapool = ctx.enter_context(tc.tile_pool(name="xapool", bufs=3))
-        xqpool = ctx.enter_context(tc.tile_pool(name="xqpool", bufs=4))
+        xqpool = ctx.enter_context(tc.tile_pool(name="xqpool", bufs=9))
         hpool = ctx.enter_context(tc.tile_pool(name="hpool", bufs=5))
         opool = ctx.enter_context(tc.tile_pool(name="opool", bufs=3))
-        ps_x = ctx.enter_context(tc.psum_pool(name="ps_x", bufs=3))
-        ps_d = ctx.enter_context(tc.psum_pool(name="ps_d", bufs=1))
-        ps_u = ctx.enter_context(tc.psum_pool(name="ps_u", bufs=1))
+        ps_x = ctx.enter_context(tc.psum_pool(name="ps_x", bufs=6))
+        ps_d = ctx.enter_context(tc.psum_pool(name="ps_d", bufs=2))
 
         ident = keep.tile([P, P], F32, name="ident", align_bytes=64)
         wd_sc = keep.tile([P, G1, 4], F32, name="wd_sc")
@@ -129,14 +133,12 @@ def tile_fp8_bottleneck_adapter_d3_kernel(tc, x, a, wd_bytes, wd_scale, g, wu_by
         osb = {}
 
         def on_vector(i):
-            if i == NT - 1:
-                return 3
-            return 1 if i % 2 == 1 and i < NT - 2 else 2
+            return NV[i]
 
         def transposes(i):
             words = xs[i][:].bitcast(F32)
             for b in range(2):
-                pt = ps_x.tile([P, 2, 2, P], F32, name="xt")
+                pt = ps_x.tile([P, 2, 2, P], F32, name="bank")
                 for u in range(2):
                     for gl in range(2):
                         q = 2 * b + gl
@@ -197,7 +199,7 @@ def tile_fp8_bottleneck_adapter_d3_kernel(tc, x, a, wd_bytes, wd_scale, g, wu_by
             hq[i] = (codes, scales)
 
         def stage2(i, c):
-            pt = ps_u.tile([P, NC], F32, name=f"u{c}")
+            pt = ps_x.tile([P, NC], F32, name="bank")
             codes, scales = hq[i]
             nc.tensor.matmul_mx(
                 out=pt[:],
@@ -234,65 +236,59 @@ def tile_fp8_bottleneck_adapter_d3_kernel(tc, x, a, wd_bytes, wd_scale, g, wu_by
             else:
                 nc.sync.dma_start(out=out[rows, base : base + 2 * NC], in_=osb[i, h][:])
 
-        def step(i):
+        def weight_op(op):
+            kind, q = op[1], int(op[2])
+            if op[0] == "w":
+                widen(kind, q, WID.get(op[1:], "S"))
+            elif op[0] == "i":
+                interleave(kind, q, IL[op[1:]])
+            else:
+                quantize_w(kind, q)
+
+        pending = S_ORDER.split()
+
+        def scalar_until(op):
+            while pending and (op is None or op in pending):
+                weight_op(pending.pop(0))
+
+        def vector_weights(s):
+            for op in V_AT.get(s, "").split():
+                if op[0] == "q":
+                    scalar_until("i" + op[1:])
+                if op[0] == "i":
+                    scalar_until("w" + op[1:])
+                weight_op(op)
+
+
+        for s in range(NT + AHEAD + LAG):
+            i = s - AHEAD
             j = i - LAG
             if 0 <= j < NT:
                 for c in range(CH):
                     stage2(j, c)
             if 0 <= i < NT:
                 stage1(i)
-            if 0 <= i + AHEAD < NT:
-                transposes(i + AHEAD)
-            k = i + AHEAD - 1
+            if s < NT:
+                transposes(s)
+            vector_weights(s)
+            k = s - 1
+
+
             if 0 <= k < NT:
                 exit_x(k, 0)
+            if 0 <= k - 1 < NT:
+                quantize_x(k - 1)
             if 0 <= j < NT:
                 exit_u(j, 0)
+            if 0 <= i - 1 < NT:
+                quantize_h(i - 1)
             if 0 <= k < NT:
                 exit_x(k, 1)
             if 0 <= j < NT:
-                exit_u(j, 1)
-                finish(j, 0)
-                exit_u(j, 2)
-                exit_u(j, 3)
+                for c in range(1, CH):
+                    exit_u(j, c)
+                    if c == 1:
+                        finish(j, 0)
                 finish(j, 1)
             if 0 <= i < NT:
                 exit_d(i)
-            if 0 <= k < NT:
-                quantize_x(k)
-            if 0 <= i < NT:
-                quantize_h(i)
-
-        widen("d", 0, "S")
-        widen("d", 1, "V")
-        interleave("d", 1, "V")
-        interleave("d", 0, "G")
-        transposes(0)
-        widen("d", 2, "S")
-        quantize_w("d", 1)
-        exit_x(0, 0)
-        exit_x(0, 1)
-        interleave("d", 2, "G")
-        transposes(1)
-        quantize_x(0)
-        quantize_w("d", 0)
-        widen("d", 3, "S")
-        exit_x(1, 0)
-        exit_x(1, 1)
-        interleave("d", 3, "V")
-        quantize_x(1)
-        quantize_w("d", 2)
-        quantize_w("d", 3)
-        transposes(2)
-        for i in range(NT + LAG):
-            if i == 0:
-                for c in range(CH):
-                    widen("u", c, "S")
-                    interleave("u", c, "S" if c == CH - 1 else "G")
-                quantize_w("u", 0)
-            if i == 1:
-                quantize_w("u", 1)
-            if i == LAG:
-                quantize_w("u", 2)
-                quantize_w("u", 3)
-            step(i)

@@ -16,6 +16,7 @@ ADD = mybir.AluOpType.add
 MULT = mybir.AluOpType.mult
 MAX = mybir.AluOpType.max
 COPY = mybir.ActivationFunctionType.Copy
+RELU = mybir.ActivationFunctionType.Relu
 
 P = 128
 NT = T // P
@@ -28,7 +29,11 @@ IL = {"d0": "V", "d1": "V", "d2": "V", "d3": "S", "u0": "S", "u1": "S", "u2": "S
 WID = {"d1": "V"}
 S_ORDER = "wd0 wd2 wd3 id3 wu0 iu0 wu1 iu1 wu2 iu2 wu3 iu3"
 V_AT = {0: "wd1 id1 id0", 2: "qd1", 4: "id2", 5: "qd2", 6: "qd0 qd3", 8: "qu0", 9: "qu1", 10: "qu2", 11: "qu3"}
-NV = [3]*12
+NV = [3, 3, 3, 3, 3, 3, 3, 3, 3, 3, 3, 3]
+DES = []
+CORD = [3, 0, 2, 1]
+BANKS = (6, 2, 0)
+S_FIRST = 0
 
 
 def tile_fp8_bottleneck_adapter_d3_kernel(tc, x, a, wd_bytes, wd_scale, g, wu_bytes, wu_scale, out):
@@ -40,15 +45,17 @@ def tile_fp8_bottleneck_adapter_d3_kernel(tc, x, a, wd_bytes, wd_scale, g, wu_by
         xapool = ctx.enter_context(tc.tile_pool(name="xapool", bufs=3))
         xqpool = ctx.enter_context(tc.tile_pool(name="xqpool", bufs=9))
         hpool = ctx.enter_context(tc.tile_pool(name="hpool", bufs=5))
-        opool = ctx.enter_context(tc.tile_pool(name="opool", bufs=3))
-        ps_x = ctx.enter_context(tc.psum_pool(name="ps_x", bufs=6))
-        ps_d = ctx.enter_context(tc.psum_pool(name="ps_d", bufs=2))
+        opool = ctx.enter_context(tc.tile_pool(name="opool", bufs=5))
+        ps_x = ctx.enter_context(tc.psum_pool(name="ps_x", bufs=BANKS[0]))
+        ps_d = ctx.enter_context(tc.psum_pool(name="ps_d", bufs=BANKS[1]))
+        ps_s = ctx.enter_context(tc.psum_pool(name="ps_s", bufs=max(BANKS[2], 1)))
 
         ident = keep.tile([P, P], F32, name="ident", align_bytes=64)
         wd_sc = keep.tile([P, G1, 4], F32, name="wd_sc")
         wu_sc = keep.tile([P, 4], F32, name="wu_sc")
         a_sb = keep.tile([P, G1, 4], BF16, name="a_sb")
         g_sb = keep.tile([P, 4], BF16, name="g_sb")
+        g_f = keep.tile([P, 4], F32, name="g_f")
         wd_raw = [keep.tile([P, 4, R], U8, name=f"wd_raw{q}", align_bytes=64) for q in range(G1)]
         wu_raw = [keep.tile([P, 4, K // 2], U8, name=f"wu_raw{q}", align_bytes=64) for q in range(2)]
         wd_q = [keep.tile([P, R], U32, name=f"wd_q{q}", align_bytes=64) for q in range(G1)]
@@ -63,6 +70,7 @@ def tile_fp8_bottleneck_adapter_d3_kernel(tc, x, a, wd_bytes, wd_scale, g, wu_by
         nc.scalar.dma_start(out=wu_sc[:], in_=wu_scale.rearrange("(p j) o -> p (j o)", j=4))
         nc.scalar.dma_start(out=g_sb[:], in_=g.rearrange("(p j) -> p j", j=4))
         make_identity(nc, ident[:])
+        nc.gpsimd.tensor_scalar(out=g_f[:], in0=g_sb[:], scalar1=1.0, scalar2=0.0, op0=MULT, op1=ADD)
 
         xs = {}
 
@@ -190,6 +198,21 @@ def tile_fp8_bottleneck_adapter_d3_kernel(tc, x, a, wd_bytes, wd_scale, g, wu_by
             )
             hg[i] = t
 
+        hp = {}
+
+        def relu_d(i):
+            r = hpool.tile([P, 4, P], F32, name="hr", align_bytes=64)
+            nc.scalar.activation(out=r[:], in_=d_ps[i][:], func=RELU)
+            t = hpool.tile([P, 4, P], BF16, name="hp", align_bytes=64)
+            for q in range(4):
+                nc.scalar.activation(out=t[:, q, :], in_=r[:, q, :], func=COPY, scale=g_f[:, q : q + 1])
+            hp[i] = t
+
+        def interleave_h(i):
+            t = hpool.tile([P, P, 4], BF16, name="hg", align_bytes=64)
+            nc.vector.tensor_copy(out=t[:], in_=hp[i][:].rearrange("p t n -> p n t"))
+            hg[i] = t
+
         def quantize_h(i):
             codes = hpool.tile([P, P], U32, name="hq", align_bytes=64)
             scales = hpool.tile([P, P], U8, name="hqs", align_bytes=64)
@@ -199,7 +222,10 @@ def tile_fp8_bottleneck_adapter_d3_kernel(tc, x, a, wd_bytes, wd_scale, g, wu_by
             hq[i] = (codes, scales)
 
         def stage2(i, c):
-            pt = ps_x.tile([P, NC], F32, name="bank")
+            if BANKS[2] and c >= on_vector(i):
+                pt = ps_s.tile([P, NC], F32, name="sbank")
+            else:
+                pt = ps_x.tile([P, NC], F32, name="bank")
             codes, scales = hq[i]
             nc.tensor.matmul_mx(
                 out=pt[:],
@@ -212,11 +238,13 @@ def tile_fp8_bottleneck_adapter_d3_kernel(tc, x, a, wd_bytes, wd_scale, g, wu_by
             )
             u_ps[i, c] = pt
 
+        def open_out(i):
+            for h in range(2):
+                osb[i, h] = opool.tile([P, 2 * NC], F32, name="o%d" % h, align_bytes=64)
+
         def exit_u(i, c):
             h = c // 2
             cols = slice(c * NC, (c + 1) * NC)
-            if c % 2 == 0:
-                osb[i, h] = opool.tile([P, 2 * NC], F32, name=f"o{h}", align_bytes=64)
             dst = osb[i, h][:, (c % 2) * NC : (c % 2 + 1) * NC]
             if c < on_vector(i):
                 nc.vector.tensor_tensor(out=dst, in0=u_ps[i, c][:], in1=xs[i][:, cols], op=ADD)
@@ -263,32 +291,47 @@ def tile_fp8_bottleneck_adapter_d3_kernel(tc, x, a, wd_bytes, wd_scale, g, wu_by
         for s in range(NT + AHEAD + LAG):
             i = s - AHEAD
             j = i - LAG
-            if 0 <= j < NT:
-                for c in range(CH):
+            k = s - 1
+            has_i, has_j, has_k = 0 <= i < NT, 0 <= j < NT, 0 <= k < NT
+            if has_j:
+                for c in CORD:
                     stage2(j, c)
-            if 0 <= i < NT:
+            if has_i:
                 stage1(i)
             if s < NT:
                 transposes(s)
             vector_weights(s)
-            k = s - 1
 
+            def u_scalar():
+                if has_j:
+                    for c in range(on_vector(j), CH):
+                        exit_u(j, c)
 
-            if 0 <= k < NT:
+            if has_j:
+                open_out(j)
+            u_scalar()
+            if 0 <= i - 1 < NT and (i - 1) in DES:
+                interleave_h(i - 1)
+            if has_k:
                 exit_x(k, 0)
             if 0 <= k - 1 < NT:
                 quantize_x(k - 1)
-            if 0 <= j < NT:
+            if has_j and on_vector(j) > 0:
                 exit_u(j, 0)
             if 0 <= i - 1 < NT:
                 quantize_h(i - 1)
-            if 0 <= k < NT:
+            if has_k:
                 exit_x(k, 1)
-            if 0 <= j < NT:
-                for c in range(1, CH):
+            if has_j:
+                for c in range(1, on_vector(j)):
                     exit_u(j, c)
                     if c == 1:
                         finish(j, 0)
+                if on_vector(j) < 2:
+                    finish(j, 0)
                 finish(j, 1)
-            if 0 <= i < NT:
-                exit_d(i)
+            if has_i:
+                if i in DES:
+                    relu_d(i)
+                else:
+                    exit_d(i)

from contextlib import ExitStack

import concourse.mybir as mybir
from concourse.masks import make_identity

T, K, R = 1536, 2048, 512
FLOPS = 2 * T * K * R * 2

F32 = mybir.dt.float32
BF16 = mybir.dt.bfloat16
U32 = mybir.dt.uint32
U8 = mybir.dt.uint8
FP8 = mybir.dt.float8_e4m3fn
FP8X4 = mybir.dt.float8_e4m3fn_x4
ADD = mybir.AluOpType.add
MULT = mybir.AluOpType.mult
MAX = mybir.AluOpType.max
COPY = mybir.ActivationFunctionType.Copy
RELU = mybir.ActivationFunctionType.Relu

P = 128
NT = T // P
G1 = K // 512
NC = 512
CH = K // NC
LAG = 4
AHEAD = 8
IL = {"d0": "V", "d1": "V", "d2": "V", "d3": "S", "u0": "S", "u1": "S", "u2": "S", "u3": "S"}
WID = {"d1": "V"}
S_ORDER = "wd0 wd2 wd3 id3 wu0 iu0 wu1 iu1 wu2 iu2 wu3 iu3"
V_AT = {0: "wd1 id1 id0", 2: "qd1", 4: "id2", 5: "qd2", 6: "qd0 qd3", 8: "qu0", 9: "qu1", 10: "qu2", 11: "qu3"}
NV = [3, 3, 3, 3, 3, 3, 3, 3, 3, 3, 3, 3]
DES = []
CORD = [3, 0, 2, 1]
BANKS = (6, 2, 0)
S_FIRST = 0


def tile_fp8_bottleneck_adapter_d3_kernel(tc, x, a, wd_bytes, wd_scale, g, wu_bytes, wu_scale, out):
    nc = tc.nc
    with ExitStack() as ctx:
        keep = ctx.enter_context(tc.tile_pool(name="keep", bufs=1))
        xpool = ctx.enter_context(tc.tile_pool(name="xpool", bufs=NT))
        wpool = ctx.enter_context(tc.tile_pool(name="wpool", bufs=4))
        xapool = ctx.enter_context(tc.tile_pool(name="xapool", bufs=3))
        xqpool = ctx.enter_context(tc.tile_pool(name="xqpool", bufs=9))
        hpool = ctx.enter_context(tc.tile_pool(name="hpool", bufs=5))
        opool = ctx.enter_context(tc.tile_pool(name="opool", bufs=5))
        ps_x = ctx.enter_context(tc.psum_pool(name="ps_x", bufs=BANKS[0]))
        ps_d = ctx.enter_context(tc.psum_pool(name="ps_d", bufs=BANKS[1]))
        ps_s = ctx.enter_context(tc.psum_pool(name="ps_s", bufs=max(BANKS[2], 1)))

        ident = keep.tile([P, P], F32, name="ident", align_bytes=64)
        wd_sc = keep.tile([P, G1, 4], F32, name="wd_sc")
        wu_sc = keep.tile([P, 4], F32, name="wu_sc")
        a_sb = keep.tile([P, G1, 4], BF16, name="a_sb")
        g_sb = keep.tile([P, 4], BF16, name="g_sb")
        g_f = keep.tile([P, 4], F32, name="g_f")
        wd_raw = [keep.tile([P, 4, R], U8, name=f"wd_raw{q}", align_bytes=64) for q in range(G1)]
        wu_raw = [keep.tile([P, 4, K // 2], U8, name=f"wu_raw{q}", align_bytes=64) for q in range(2)]
        wd_q = [keep.tile([P, R], U32, name=f"wd_q{q}", align_bytes=64) for q in range(G1)]
        wd_s = [keep.tile([P, R], U8, name=f"wd_s{q}", align_bytes=64) for q in range(G1)]
        wu_q = [keep.tile([P, NC], U32, name=f"wu_q{q}", align_bytes=64) for q in range(CH)]
        wu_s = [keep.tile([P, NC], U8, name=f"wu_s{q}", align_bytes=64) for q in range(CH)]

        ctx.enter_context(tc.manual_schedule())

        nc.scalar.dma_start(out=wd_sc[:], in_=wd_scale.rearrange("(g p j) o -> p g (j o)", p=P, j=4))
        nc.scalar.dma_start(out=a_sb[:], in_=a.rearrange("(g p j) -> p g j", p=P, j=4))
        nc.scalar.dma_start(out=wu_sc[:], in_=wu_scale.rearrange("(p j) o -> p (j o)", j=4))
        nc.scalar.dma_start(out=g_sb[:], in_=g.rearrange("(p j) -> p j", j=4))
        make_identity(nc, ident[:])
        nc.gpsimd.tensor_scalar(out=g_f[:], in0=g_sb[:], scalar1=1.0, scalar2=0.0, op0=MULT, op1=ADD)

        xs = {}

        def load_x(i):
            t = xpool.tile([P, K], BF16, name="xt_in", align_bytes=64)
            nc.sync.dma_start(out=t[:], in_=x[i * P : (i + 1) * P, :])
            xs[i] = t

        wd_view = wd_bytes.rearrange("(g p j) r -> g p j r", p=P, j=4)
        wu_view = wu_bytes.rearrange("(p j) n -> p j n", j=4)
        for q in range(G1):
            nc.sync.dma_start(out=wd_raw[q][:], in_=wd_view[q])
        load_x(0)
        nc.sync.dma_start(out=wu_raw[0][:], in_=wu_view[:, :, 0 : K // 2])
        load_x(1)
        nc.sync.dma_start(out=wu_raw[1][:], in_=wu_view[:, :, K // 2 : K])
        for i in range(2, NT):
            load_x(i)

        wide = {}
        grp = {}

        def widen(kind, q, eng):
            t = wpool.tile([P, 4, NC], BF16, name="wide", align_bytes=64)
            for j in range(4):
                if kind == "d":
                    src, sc = wd_raw[q][:, j, :], wd_sc[:, q, j : j + 1]
                else:
                    src, sc = wu_raw[q // 2][:, j, (q % 2) * NC : (q % 2 + 1) * NC], wu_sc[:, j : j + 1]
                src = src.bitcast(FP8)
                if eng == "S":
                    nc.scalar.activation(out=t[:, j, :], in_=src, func=COPY, scale=sc)
                else:
                    nc.vector.tensor_scalar(out=t[:, j, :], in0=src, scalar1=sc, scalar2=None, op0=MULT)
            wide[kind, q] = t

        def interleave(kind, q, eng):
            t = wpool.tile([P, NC, 4], BF16, name="grp", align_bytes=64)
            if kind == "d":
                dst = t[:].rearrange("p (t m) j -> p t m j", t=4)
                src = wide[kind, q][:].rearrange("p j (m t) -> p t m j", t=4)
            else:
                dst = t[:]
                src = wide[kind, q][:].rearrange("p j n -> p n j")
            if eng == "V":
                nc.vector.tensor_copy(out=dst, in_=src)
            elif eng == "S":
                nc.scalar.copy(out=dst, in_=src)
            else:
                nc.gpsimd.tensor_scalar(out=dst, in0=src, scalar1=1.0, scalar2=0.0, op0=MULT, op1=ADD)
            grp[kind, q] = t

        def quantize_w(kind, q):
            codes, scales = (wd_q[q], wd_s[q]) if kind == "d" else (wu_q[q], wu_s[q])
            nc.vector.quantize_mx(
                out=codes[:].bitcast(FP8X4),
                scales=scales[:],
                in_=grp[kind, q][:].rearrange("p n j -> p (n j)"),
            )

        xt_ps = {}
        xa = {}
        xq = {}
        d_ps = {}
        hg = {}
        hq = {}
        u_ps = {}
        osb = {}

        def on_vector(i):
            return NV[i]

        def transposes(i):
            words = xs[i][:].bitcast(F32)
            for b in range(2):
                pt = ps_x.tile([P, 2, 2, P], F32, name="bank")
                for u in range(2):
                    for gl in range(2):
                        q = 2 * b + gl
                        nc.tensor.transpose(pt[:, u, gl, :], words[:, 256 * q + u : 256 * (q + 1) : 2], ident[:])
                xt_ps[i, b] = pt

        def exit_x(i, b):
            if b == 0:
                xa[i] = xapool.tile([P, G1, P, 2, 2], BF16, name="xa", align_bytes=64)
            src = xt_ps[i, b][:].rearrange("p u g r -> p (u g r)").bitcast(BF16).rearrange("p (u g r e) -> p g r u e", u=2, g=2, e=2)
            fac = a_sb[:, 2 * b : 2 * b + 2, :].rearrange("p g (u e) -> p g u e", e=2).unsqueeze(2).to_broadcast([P, 2, P, 2, 2])
            nc.vector.tensor_tensor(out=xa[i][:, 2 * b : 2 * b + 2], in0=src, in1=fac, op=MULT)

        def quantize_x(i):
            codes = xqpool.tile([P, G1, P], U32, name="xq", align_bytes=64)
            scales = xqpool.tile([P, G1, P], U8, name="xqs", align_bytes=64)
            nc.vector.quantize_mx(
                out=codes[:].rearrange("p g r -> p (g r)").bitcast(FP8X4),
                scales=scales[:].rearrange("p g r -> p (g r)"),
                in_=xa[i][:].rearrange("p g r u e -> p (g r u e)"),
            )
            xq[i] = (codes, scales)

        def stage1(i):
            pt = ps_d.tile([P, 4, P], F32, name="d")
            codes, scales = xq[i]
            for t in range(4):
                for q in range(G1):
                    nc.tensor.matmul_mx(
                        out=pt[:, t, :],
                        lhsT=wd_q[q][:, t * P : (t + 1) * P].bitcast(FP8X4),
                        lhsT_scale=wd_s[q][:, t * P : (t + 1) * P],
                        rhs=codes[:, q, :].bitcast(FP8X4),
                        rhs_scale=scales[:, q, :],
                        start=(q == 0),
                        stop=(q == G1 - 1),
                    )
            d_ps[i] = pt

        def exit_d(i):
            t = hpool.tile([P, P, 4], BF16, name="hg", align_bytes=64)
            nc.vector.scalar_tensor_tensor(
                out=t[:],
                in0=d_ps[i][:].rearrange("p t n -> p n t"),
                scalar=0.0,
                in1=g_sb[:].unsqueeze(1).to_broadcast([P, P, 4]),
                op0=MAX,
                op1=MULT,
            )
            hg[i] = t

        hp = {}

        def relu_d(i):
            r = hpool.tile([P, 4, P], F32, name="hr", align_bytes=64)
            nc.scalar.activation(out=r[:], in_=d_ps[i][:], func=RELU)
            t = hpool.tile([P, 4, P], BF16, name="hp", align_bytes=64)
            for q in range(4):
                nc.scalar.activation(out=t[:, q, :], in_=r[:, q, :], func=COPY, scale=g_f[:, q : q + 1])
            hp[i] = t

        def interleave_h(i):
            t = hpool.tile([P, P, 4], BF16, name="hg", align_bytes=64)
            nc.vector.tensor_copy(out=t[:], in_=hp[i][:].rearrange("p t n -> p n t"))
            hg[i] = t

        def quantize_h(i):
            codes = hpool.tile([P, P], U32, name="hq", align_bytes=64)
            scales = hpool.tile([P, P], U8, name="hqs", align_bytes=64)
            nc.vector.quantize_mx(
                out=codes[:].bitcast(FP8X4), scales=scales[:], in_=hg[i][:].rearrange("p n t -> p (n t)")
            )
            hq[i] = (codes, scales)

        def stage2(i, c):
            if BANKS[2] and c >= on_vector(i):
                pt = ps_s.tile([P, NC], F32, name="sbank")
            else:
                pt = ps_x.tile([P, NC], F32, name="bank")
            codes, scales = hq[i]
            nc.tensor.matmul_mx(
                out=pt[:],
                lhsT=codes[:].bitcast(FP8X4),
                lhsT_scale=scales[:],
                rhs=wu_q[c][:].bitcast(FP8X4),
                rhs_scale=wu_s[c][:],
                start=True,
                stop=True,
            )
            u_ps[i, c] = pt

        def open_out(i):
            for h in range(2):
                osb[i, h] = opool.tile([P, 2 * NC], F32, name="o%d" % h, align_bytes=64)

        def exit_u(i, c):
            h = c // 2
            cols = slice(c * NC, (c + 1) * NC)
            dst = osb[i, h][:, (c % 2) * NC : (c % 2 + 1) * NC]
            if c < on_vector(i):
                nc.vector.tensor_tensor(out=dst, in0=u_ps[i, c][:], in1=xs[i][:, cols], op=ADD)
            else:
                nc.scalar.copy(out=dst, in_=u_ps[i, c][:])

        def finish(i, h):
            lo = max(on_vector(i) - 2 * h, 0) * NC
            base = h * 2 * NC
            if lo < 2 * NC:
                part = osb[i, h][:, lo : 2 * NC]
                nc.gpsimd.tensor_tensor(out=part, in0=part, in1=xs[i][:, base + lo : base + 2 * NC], op=ADD)
            rows = slice(i * P, (i + 1) * P)
            if i == NT - 1:
                for s in range(0, 2 * NC, NC):
                    nc.sync.dma_start(out=out[rows, base + s : base + s + NC], in_=osb[i, h][:, s : s + NC])
            else:
                nc.sync.dma_start(out=out[rows, base : base + 2 * NC], in_=osb[i, h][:])

        def weight_op(op):
            kind, q = op[1], int(op[2])
            if op[0] == "w":
                widen(kind, q, WID.get(op[1:], "S"))
            elif op[0] == "i":
                interleave(kind, q, IL[op[1:]])
            else:
                quantize_w(kind, q)

        pending = S_ORDER.split()

        def scalar_until(op):
            while pending and (op is None or op in pending):
                weight_op(pending.pop(0))

        def vector_weights(s):
            for op in V_AT.get(s, "").split():
                if op[0] == "q":
                    scalar_until("i" + op[1:])
                if op[0] == "i":
                    scalar_until("w" + op[1:])
                weight_op(op)


        for s in range(NT + AHEAD + LAG):
            i = s - AHEAD
            j = i - LAG
            k = s - 1
            has_i, has_j, has_k = 0 <= i < NT, 0 <= j < NT, 0 <= k < NT
            if has_j:
                for c in CORD:
                    stage2(j, c)
            if has_i:
                stage1(i)
            if s < NT:
                transposes(s)
            vector_weights(s)

            def u_scalar():
                if has_j:
                    for c in range(on_vector(j), CH):
                        exit_u(j, c)

            if has_j:
                open_out(j)
            u_scalar()
            if 0 <= i - 1 < NT and (i - 1) in DES:
                interleave_h(i - 1)
            if has_k:
                exit_x(k, 0)
            if 0 <= k - 1 < NT:
                quantize_x(k - 1)
            if has_j and on_vector(j) > 0:
                exit_u(j, 0)
            if 0 <= i - 1 < NT:
                quantize_h(i - 1)
            if has_k:
                exit_x(k, 1)
            if has_j:
                for c in range(1, on_vector(j)):
                    exit_u(j, c)
                    if c == 1:
                        finish(j, 0)
                if on_vector(j) < 2:
                    finish(j, 0)
                finish(j, 1)
            if has_i:
                if i in DES:
                    relu_d(i)
                else:
                    exit_d(i)
